import numpy as np
import ml_dtypes


def mxq(x, axis, fmt="e4m3"):
    dtype, down = {"e4m3": (ml_dtypes.float8_e4m3fn, 7), "e5m2": (ml_dtypes.float8_e5m2, 14)}[fmt]
    v = np.moveaxis(np.asarray(x, np.float32).astype(ml_dtypes.bfloat16).astype(np.float64), axis, -1)
    blocks = v.reshape(v.shape[:-1] + (-1, 32))
    amax = np.abs(blocks).max(-1, keepdims=True)
    byte = np.maximum(np.where(amax > 0, np.frexp(amax)[1] - 1 + 127, 0) - down, 1)
    scale = np.exp2(byte - 127.0)
    codes = (blocks / scale).astype(np.float32).astype(dtype).astype(np.float64)
    return np.moveaxis((codes * scale).reshape(v.shape), -1, axis)


WIDE = False


def mx_kscale(k):
    if not WIDE:
        return np.ones(k)
    levels = np.array([30, -30])
    if k % 512:
        return np.exp2(np.random.permutation(np.resize(levels, k // 32))).repeat(32)
    a = np.empty((k // 512, 16))
    for p in range(k // 512):
        a[p, :8] = np.random.permutation(np.resize(levels, 8))
        for g in range(8):
            far = levels[np.abs(levels - a[p, g]) >= 10]
            a[p, g + 8] = far[np.random.randint(len(far))]
    return np.exp2(a.ravel()).repeat(32)


def f64(x):
    return np.asarray(x).astype(np.float64)


def striped(idx):
    return np.tile(np.asarray(idx).reshape(-1, 16).T, (8, 1)).astype(np.uint16)


def unstriped(offs):
    return offs[:16].T.reshape(-1).astype(np.int64)


E2M1 = np.array([0.0, 0.5, 1.0, 1.5, 2.0, 3.0, 4.0, 6.0, -0.0, -0.5, -1.0, -1.5, -2.0, -3.0, -4.0, -6.0])


def pack_weight(w, fmt):
    k, n = w.shape
    w = f64(np.asarray(w, np.float32).astype(ml_dtypes.bfloat16)).reshape(k // 32, 32, n)
    amax = np.abs(w).max(1)
    if fmt == "e4m3":
        byte = np.frexp(amax)[1] - 1 + 127 - 7
    else:
        mant, ex = np.frexp(amax / 6.0)
        byte = np.where(mant > 0.5, ex, ex - 1) + 127
    byte = np.clip(np.where(amax > 0, byte, 1), 1, 254)
    scaled = (w * np.exp2(127.0 - byte)[:, None, :]).reshape(k, n).astype(np.float32)
    by_word = np.ascontiguousarray(scaled.reshape(k // 512, 128, 4, n).transpose(0, 1, 3, 2))
    if fmt == "e4m3":
        words = by_word.astype(ml_dtypes.float8_e4m3fn).view(np.uint8)
    else:
        c = by_word.astype(ml_dtypes.float4_e2m1fn).view(np.uint8) & 0xF
        words = (c[..., 0::2] | (c[..., 1::2] << 4)).reshape(k // 512, 128, 2 * n)
    return np.ascontiguousarray(words), np.ascontiguousarray(byte.astype(np.uint8).reshape(k // 512, 16, n))


def unpack_weight(words, scales, fmt):
    g, _, n = scales.shape
    words = np.ascontiguousarray(words).reshape(g, 128, n, -1)
    if fmt == "e4m3":
        vals = words.view(ml_dtypes.float8_e4m3fn).astype(np.float64)
    else:
        nib = np.empty((g, 128, n, 4), np.uint8)
        nib[..., 0::2] = words & 0xF
        nib[..., 1::2] = words >> 4
        vals = E2M1[nib]
    vals = vals * np.repeat(np.exp2(scales.astype(np.float64) - 127.0), 8, axis=1)[..., None]
    return vals.transpose(0, 1, 3, 2).reshape(g * 512, n)


K, J, T, N = 2048, 512, 512, 512


def setup_inputs():
    n = np.random.standard_normal
    idx = np.random.permutation(K)[:J]
    fk = mx_kscale(K)
    fj = mx_kscale(J)
    tj = np.ones(K)
    tj[idx] = fj
    xo = n((T, K)) * np.exp(0.5 * n((T, 1)))
    xo[:, idx] *= 4.0
    xr = xo.copy()
    xr[:, idx] = 0.0
    gbp = pack_weight(xr.T / fk[:, None], "e2m1")
    wbp = pack_weight(n((K, N)) * 1 / np.sqrt(K) * fk[:, None], "e4m3")
    wop = pack_weight(n((J, N)) * 1 / np.sqrt(J) * fj[:, None], "e2m1")
    return {
        "gb_words": gbp[0],
        "gb_scales": gbp[1],
        "wb_words": wbp[0],
        "wb_scales": wbp[1],
        "gt": (xo / tj).astype(np.float32),
        "wo_words": wop[0],
        "wo_scales": wop[1],
        "res": (1.0 * n((N, T))).astype(np.float32),
        "ls": (np.random.uniform(0.25, 1.5, (N, 1))).astype(np.float32),
        "offs": striped(idx),
    }


def reference(gb_words, gb_scales, wb_words, wb_scales, gt, wo_words, wo_scales, res, ls, offs):
    idx = unstriped(offs)
    gbu = unpack_weight(gb_words, gb_scales, "e2m1")
    wbu = unpack_weight(wb_words, wb_scales, "e4m3")
    wou = unpack_weight(wo_words, wo_scales, "e2m1")
    gl = f64(gt)[:, idx].T
    glq = mxq(gl, 0, "e5m2")
    z = wbu.T @ gbu + wou.T @ glq
    y = z * f64(ls) + f64(res)
    return y

@@ -1,0 +1,144 @@
+from contextlib import ExitStack
+
+import concourse.mybir as mybir
+from concourse.masks import make_identity
+
+K, J, T, N = 2048, 512, 512, 512
+FLOPS = 2 * (K + J) * T * N
+
+F32 = mybir.dt.float32
+BF16 = mybir.dt.bfloat16
+I32 = mybir.dt.int32
+U32 = mybir.dt.uint32
+U16 = mybir.dt.uint16
+U8 = mybir.dt.uint8
+E4M3X4 = mybir.dt.float8_e4m3fn_x4
+E5M2X4 = mybir.dt.float8_e5m2_x4
+E2M1X4 = mybir.dt.float4_e2m1fn_x4
+MULT = mybir.AluOpType.mult
+ADD = mybir.AluOpType.add
+
+P = 128
+PASSES = K // 512
+TILES = T // P
+BANKS = N // P
+EARLY = 2
+
+
+def tile_list_outlier_gradient_kernel(tc, gb_words, gb_scales, wb_words, wb_scales, gt, wo_words, wo_scales, res, ls, offs, out):
+    nc = tc.nc
+    with ExitStack() as ctx:
+        keep = ctx.enter_context(tc.tile_pool(name="keep", bufs=1))
+        psum = ctx.enter_context(tc.psum_pool(name="psum", bufs=1))
+
+        offsets = keep.tile([P, J // 16], U16, name="offsets")
+        rows = [keep.tile([P, K], F32, name=f"rows{i}") for i in range(TILES)]
+        wb_early = keep.tile([P, EARLY, N], I32, name="wb_early", align_bytes=64)
+        wb_late = [keep.tile([P, 1, N], I32, name=f"wb_late{z}", align_bytes=64) for z in range(EARLY, PASSES)]
+        gb_early = keep.tile([P, EARLY, 2 * T], U8, name="gb_early", align_bytes=64)
+        gb_late = keep.tile([P, PASSES - EARLY, 2 * T], U8, name="gb_late", align_bytes=64)
+        wo_sb = keep.tile([P, 2 * N], U8, name="wo_sb", align_bytes=64)
+        wb_sc = keep.tile([P, PASSES, N], U8, name="wb_sc", align_bytes=64)
+        gb_sc = keep.tile([P, PASSES, T], U8, name="gb_sc", align_bytes=64)
+        wo_sc = keep.tile([P, 1, N], U8, name="wo_sc", align_bytes=64)
+        res_sb = [keep.tile([P, T], F32, name=f"res{b}") for b in range(BANKS)]
+        ls_rows = keep.tile([P, P], F32, name="ls_rows")
+        ls_cols = keep.tile([P, BANKS], F32, name="ls_cols")
+        ident = keep.tile([P, P], F32, name="ident")
+        codes = keep.tile([P, T], U32, name="codes", align_bytes=64)
+        gl_sc = keep.tile([P, T], U8, name="gl_sc", align_bytes=64)
+        acc = [psum.tile([P, T], F32, name=f"acc{b}") for b in range(BANKS)]
+
+        nc.gpsimd.memset(wb_sc[:].bitcast(I32), 0)
+        nc.vector.memset(gb_sc[:].bitcast(I32), 0)
+        nc.gpsimd.memset(wo_sc[:].bitcast(I32), 0)
+        nc.gpsimd.memset(ls_rows[:], 0.0)
+        make_identity(nc, ident[:])
+
+        def load_rows(i):
+            nc.sync.dma_start(rows[i][:], gt[P * i : P * (i + 1), :])
+
+        def load_scales(queue, plane, src, r):
+            queue.dma_start(plane[r:P:32].bitcast(I32), src[:, r:16:4, :].rearrange("z q c -> q z c").bitcast(I32))
+
+        def load_wb(tile, z0, z1):
+            nc.sync.dma_start(tile[:], wb_words[z0:z1].rearrange("z p n t -> p z (n t)").bitcast(I32))
+
+        def load_gb(tile, z0, z1):
+            nc.sync.dma_start(tile[:].bitcast(I32), gb_words[z0:z1].rearrange("z p c -> p z c").bitcast(I32))
+
+        load_rows(0)
+        nc.sync.dma_start(offsets[:], offs)
+        for r in range(2):
+            load_scales(nc.sync, wb_sc, wb_scales, r)
+        load_rows(1)
+        for r in range(2, 4):
+            load_scales(nc.sync, wb_sc, wb_scales, r)
+        load_scales(nc.sync, gb_sc, gb_scales, 0)
+        load_rows(2)
+        for r in range(1, 4):
+            load_scales(nc.sync, gb_sc, gb_scales, r)
+        load_gb(gb_early, 0, EARLY)
+        load_wb(wb_early, 0, EARLY)
+        load_rows(3)
+        load_gb(gb_late, EARLY, PASSES)
+        for z in range(EARLY, PASSES):
+            load_wb(wb_late[z - EARLY], z, z + 1)
+        nc.sync.dma_start(wo_sb[:].bitcast(I32), wo_words[0].bitcast(I32))
+        for b in range(BANKS):
+            nc.sync.dma_start(res_sb[b][:], res[P * b : P * (b + 1), :])
+        nc.gpsimd.dma_start(ls_rows[8 : 8 + BANKS, :], ls.rearrange("(b c) o -> b (c o)", b=BANKS))
+        for r in range(4):
+            load_scales(nc.gpsimd, wo_sc, wo_scales, r)
+
+        def listed(i):
+            picked = keep.tile([P, J], BF16, name=f"picked{i}")
+            nc.vector.tensor_copy(picked[:], rows[i][:].indirect(offsets[:]))
+            pairs = picked[:].bitcast(F32)
+            turned = psum.tile([P, 2, P], F32, name=f"turned{i % 2}")
+            for u in range(2):
+                nc.tensor.transpose(turned[:, u, :], pairs[:, u : J // 2 : 2], ident[:])
+            woven = keep.tile([P, 4 * P], BF16, name=f"woven{i}", align_bytes=64)
+            nc.scalar.copy(woven[:].bitcast(F32).rearrange("p (r u) -> p r u", u=2), turned[:].rearrange("p u r -> p r u"))
+            cols = slice(P * i, P * (i + 1))
+            nc.vector.quantize_mx(out=codes[:, cols].bitcast(E5M2X4), scales=gl_sc[:, cols], in_=woven[:])
+
+        def base_matmul(z, b):
+            words = wb_early[:, z, :] if z < EARLY else wb_late[z - EARLY][:, 0, :]
+            moving = gb_early[:, z, :] if z < EARLY else gb_late[:, z - EARLY, :]
+            cols = slice(P * b, P * (b + 1))
+            nc.tensor.matmul_mx(
+                out=acc[b][:],
+                lhsT=words[:, cols].bitcast(E4M3X4),
+                lhsT_scale=wb_sc[:, z, cols],
+                rhs=moving.bitcast(E2M1X4),
+                rhs_scale=gb_sc[:, z, :],
+                start=(z == 0),
+                stop=False,
+            )
+
+        for i in range(TILES):
+            listed(i)
+        ls_turned = psum.tile([P, P], F32, name="ls_turned")
+        nc.tensor.transpose(ls_turned[:], ls_rows[:], ident[:])
+        nc.scalar.copy(ls_cols[:], ls_turned[:, 8 : 8 + BANKS])
+        for z in range(EARLY):
+            for b in range(BANKS):
+                base_matmul(z, b)
+
+        for b in range(BANKS):
+            cols = slice(P * b, P * (b + 1))
+            for z in range(EARLY, PASSES):
+                base_matmul(z, b)
+            nc.tensor.matmul_mx(
+                out=acc[b][:],
+                lhsT=wo_sb[:, 2 * P * b : 2 * P * (b + 1)].bitcast(E2M1X4),
+                lhsT_scale=wo_sc[:, 0, cols],
+                rhs=codes[:].bitcast(E5M2X4),
+                rhs_scale=gl_sc[:],
+                start=False,
+                stop=True,
+            )
+            result = keep.tile([P, T], F32, name=f"result{b}")
+            nc.vector.scalar_tensor_tensor(result[:], acc[b][:], ls_cols[:, b : b + 1], res_sb[b][:], MULT, ADD)
+            nc.sync.dma_start(out[cols, :], result[:])

@@ -33,10 +33,8 @@ def tile_list_outlier_gradient_kernel(tc, gb_words, gb_scales, wb_words, wb_scal
 
         offsets = keep.tile([P, J // 16], U16, name="offsets")
         rows = [keep.tile([P, K], F32, name=f"rows{i}") for i in range(TILES)]
-        wb_early = keep.tile([P, EARLY, N], I32, name="wb_early", align_bytes=64)
-        wb_late = [keep.tile([P, 1, N], I32, name=f"wb_late{z}", align_bytes=64) for z in range(EARLY, PASSES)]
-        gb_early = keep.tile([P, EARLY, 2 * T], U8, name="gb_early", align_bytes=64)
-        gb_late = keep.tile([P, PASSES - EARLY, 2 * T], U8, name="gb_late", align_bytes=64)
+        wb_sb = [keep.tile([P, N], I32, name=f"wb{z}", align_bytes=64) for z in range(PASSES)]
+        gb_sb = [keep.tile([P, 2 * T], U8, name=f"gb{z}", align_bytes=64) for z in range(PASSES)]
         wo_sb = keep.tile([P, 2 * N], U8, name="wo_sb", align_bytes=64)
         wb_sc = keep.tile([P, PASSES, N], U8, name="wb_sc", align_bytes=64)
         gb_sc = keep.tile([P, PASSES, T], U8, name="gb_sc", align_bytes=64)
@@ -51,8 +49,8 @@ def tile_list_outlier_gradient_kernel(tc, gb_words, gb_scales, wb_words, wb_scal
 
         nc.gpsimd.memset(wb_sc[:].bitcast(I32), 0)
         nc.vector.memset(gb_sc[:].bitcast(I32), 0)
-        nc.gpsimd.memset(wo_sc[:].bitcast(I32), 0)
-        nc.gpsimd.memset(ls_rows[:], 0.0)
+        nc.vector.memset(ls_rows[:], 0.0)
+        nc.vector.memset(wo_sc[:].bitcast(I32), 0)
         make_identity(nc, ident[:])
 
         def load_rows(i):
@@ -61,29 +59,24 @@ def tile_list_outlier_gradient_kernel(tc, gb_words, gb_scales, wb_words, wb_scal
         def load_scales(queue, plane, src, r):
             queue.dma_start(plane[r:P:32].bitcast(I32), src[:, r:16:4, :].rearrange("z q c -> q z c").bitcast(I32))
 
-        def load_wb(tile, z0, z1):
-            nc.sync.dma_start(tile[:], wb_words[z0:z1].rearrange("z p n t -> p z (n t)").bitcast(I32))
+        def load_base(z):
+            nc.sync.dma_start(gb_sb[z][:].bitcast(I32), gb_words[z].bitcast(I32))
+            nc.sync.dma_start(wb_sb[z][:], wb_words[z].rearrange("p n t -> p (n t)").bitcast(I32))
 
-        def load_gb(tile, z0, z1):
-            nc.sync.dma_start(tile[:].bitcast(I32), gb_words[z0:z1].rearrange("z p c -> p z c").bitcast(I32))
-
-        load_rows(0)
-        nc.sync.dma_start(offsets[:], offs)
-        for r in range(2):
+        for r in range(4):
             load_scales(nc.sync, wb_sc, wb_scales, r)
-        load_rows(1)
-        for r in range(2, 4):
-            load_scales(nc.sync, wb_sc, wb_scales, r)
-        load_scales(nc.sync, gb_sc, gb_scales, 0)
-        load_rows(2)
-        for r in range(1, 4):
+        for r in range(3):
             load_scales(nc.sync, gb_sc, gb_scales, r)
-        load_gb(gb_early, 0, EARLY)
-        load_wb(wb_early, 0, EARLY)
+        load_rows(0)
+        load_scales(nc.sync, gb_sc, gb_scales, 3)
+        nc.sync.dma_start(offsets[:], offs)
+        load_rows(1)
+        load_base(0)
+        load_rows(2)
+        load_base(1)
         load_rows(3)
-        load_gb(gb_late, EARLY, PASSES)
-        for z in range(EARLY, PASSES):
-            load_wb(wb_late[z - EARLY], z, z + 1)
+        load_base(2)
+        load_base(3)
         nc.sync.dma_start(wo_sb[:].bitcast(I32), wo_words[0].bitcast(I32))
         for b in range(BANKS):
             nc.sync.dma_start(res_sb[b][:], res[P * b : P * (b + 1), :])
@@ -104,14 +97,12 @@ def tile_list_outlier_gradient_kernel(tc, gb_words, gb_scales, wb_words, wb_scal
             nc.vector.quantize_mx(out=codes[:, cols].bitcast(E5M2X4), scales=gl_sc[:, cols], in_=woven[:])
 
         def base_matmul(z, b):
-            words = wb_early[:, z, :] if z < EARLY else wb_late[z - EARLY][:, 0, :]
-            moving = gb_early[:, z, :] if z < EARLY else gb_late[:, z - EARLY, :]
             cols = slice(P * b, P * (b + 1))
             nc.tensor.matmul_mx(
                 out=acc[b][:],
-                lhsT=words[:, cols].bitcast(E4M3X4),
+                lhsT=wb_sb[z][:, cols].bitcast(E4M3X4),
                 lhsT_scale=wb_sc[:, z, cols],
-                rhs=moving.bitcast(E2M1X4),
+                rhs=gb_sb[z][:].bitcast(E2M1X4),
                 rhs_scale=gb_sc[:, z, :],
                 start=(z == 0),
                 stop=False,

@@ -59,19 +59,29 @@ def tile_list_outlier_gradient_kernel(tc, gb_words, gb_scales, wb_words, wb_scal
         def load_scales(queue, plane, src, r):
             queue.dma_start(plane[r:P:32].bitcast(I32), src[:, r:16:4, :].rearrange("z q c -> q z c").bitcast(I32))
 
-        def load_base(z):
-            nc.sync.dma_start(gb_sb[z][:].bitcast(I32), gb_words[z].bitcast(I32))
+        def load_wb(z):
             nc.sync.dma_start(wb_sb[z][:], wb_words[z].rearrange("p n t -> p (n t)").bitcast(I32))
 
-        for r in range(4):
+        def load_gb(z):
+            nc.sync.dma_start(gb_sb[z][:].bitcast(I32), gb_words[z].bitcast(I32))
+
+        def load_base(z):
+            load_wb(z)
+            load_gb(z)
+
+        load_wb(0)
+        for r in range(2):
             load_scales(nc.sync, wb_sc, wb_scales, r)
-        for r in range(3):
-            load_scales(nc.sync, gb_sc, gb_scales, r)
+        load_gb(0)
         load_rows(0)
-        load_scales(nc.sync, gb_sc, gb_scales, 3)
         nc.sync.dma_start(offsets[:], offs)
+        for r in range(2, 4):
+            load_scales(nc.sync, wb_sc, wb_scales, r)
+        for r in range(2):
+            load_scales(nc.sync, gb_sc, gb_scales, r)
         load_rows(1)
-        load_base(0)
+        for r in range(2, 4):
+            load_scales(nc.sync, gb_sc, gb_scales, r)
         load_rows(2)
         load_base(1)
         load_rows(3)
@@ -84,6 +94,8 @@ def tile_list_outlier_gradient_kernel(tc, gb_words, gb_scales, wb_words, wb_scal
         for r in range(4):
             load_scales(nc.gpsimd, wo_sc, wo_scales, r)
 
+        woven = [keep.tile([P, 2, 4 * P], BF16, name=f"woven{h}", align_bytes=64) for h in range(TILES // 2)]
+
         def listed(i):
             picked = keep.tile([P, J], BF16, name=f"picked{i}")
             nc.vector.tensor_copy(picked[:], rows[i][:].indirect(offsets[:]))
@@ -91,10 +103,11 @@ def tile_list_outlier_gradient_kernel(tc, gb_words, gb_scales, wb_words, wb_scal
             turned = psum.tile([P, 2, P], F32, name=f"turned{i % 2}")
             for u in range(2):
                 nc.tensor.transpose(turned[:, u, :], pairs[:, u : J // 2 : 2], ident[:])
-            woven = keep.tile([P, 4 * P], BF16, name=f"woven{i}", align_bytes=64)
-            nc.scalar.copy(woven[:].bitcast(F32).rearrange("p (r u) -> p r u", u=2), turned[:].rearrange("p u r -> p r u"))
-            cols = slice(P * i, P * (i + 1))
-            nc.vector.quantize_mx(out=codes[:, cols].bitcast(E5M2X4), scales=gl_sc[:, cols], in_=woven[:])
+            half = woven[i // 2]
+            nc.scalar.copy(half[:, i % 2, :].bitcast(F32).rearrange("p (r u) -> p r u", u=2), turned[:].rearrange("p u r -> p r u"))
+            if i % 2 == 1:
+                cols = slice(P * (i - 1), P * (i + 1))
+                nc.vector.quantize_mx(out=codes[:, cols].bitcast(E5M2X4), scales=gl_sc[:, cols], in_=half[:].rearrange("p a c -> p (a c)"))
 
         def base_matmul(z, b):
             cols = slice(P * b, P * (b + 1))
@@ -130,6 +143,10 @@ def tile_list_outlier_gradient_kernel(tc, gb_words, gb_scales, wb_words, wb_scal
                 start=False,
                 stop=True,
             )
-            result = keep.tile([P, T], F32, name=f"result{b}")
-            nc.vector.scalar_tensor_tensor(result[:], acc[b][:], ls_cols[:, b : b + 1], res_sb[b][:], MULT, ADD)
-            nc.sync.dma_start(out[cols, :], result[:])
+            pieces = 2 if b in (0, BANKS - 1) else 1
+            width = T // pieces
+            for h in range(pieces):
+                tok = slice(width * h, width * (h + 1))
+                result = keep.tile([P, width], F32, name=f"result{b}_{h}")
+                nc.vector.scalar_tensor_tensor(result[:], acc[b][:, tok], ls_cols[:, b : b + 1], res_sb[b][:, tok], MULT, ADD)
+                nc.sync.dma_start(out[cols, tok], result[:])

from contextlib import ExitStack

import concourse.mybir as mybir
from concourse.masks import make_identity

K, J, T, N = 2048, 512, 512, 512
FLOPS = 2 * (K + J) * T * N

F32 = mybir.dt.float32
BF16 = mybir.dt.bfloat16
I32 = mybir.dt.int32
U32 = mybir.dt.uint32
U16 = mybir.dt.uint16
U8 = mybir.dt.uint8
E4M3X4 = mybir.dt.float8_e4m3fn_x4
E5M2X4 = mybir.dt.float8_e5m2_x4
E2M1X4 = mybir.dt.float4_e2m1fn_x4
MULT = mybir.AluOpType.mult
ADD = mybir.AluOpType.add

P = 128
PASSES = K // 512
TILES = T // P
BANKS = N // P
EARLY = 2


def tile_list_outlier_gradient_kernel(tc, gb_words, gb_scales, wb_words, wb_scales, gt, wo_words, wo_scales, res, ls, offs, out):
    nc = tc.nc
    with ExitStack() as ctx:
        keep = ctx.enter_context(tc.tile_pool(name="keep", bufs=1))
        psum = ctx.enter_context(tc.psum_pool(name="psum", bufs=1))

        offsets = keep.tile([P, J // 16], U16, name="offsets")
        rows = [keep.tile([P, K], F32, name=f"rows{i}") for i in range(TILES)]
        wb_sb = [keep.tile([P, N], I32, name=f"wb{z}", align_bytes=64) for z in range(PASSES)]
        gb_sb = [keep.tile([P, 2 * T], U8, name=f"gb{z}", align_bytes=64) for z in range(PASSES)]
        wo_sb = keep.tile([P, 2 * N], U8, name="wo_sb", align_bytes=64)
        wb_sc = keep.tile([P, PASSES, N], U8, name="wb_sc", align_bytes=64)
        gb_sc = keep.tile([P, PASSES, T], U8, name="gb_sc", align_bytes=64)
        wo_sc = keep.tile([P, 1, N], U8, name="wo_sc", align_bytes=64)
        res_sb = [keep.tile([P, T], F32, name=f"res{b}") for b in range(BANKS)]
        ls_rows = keep.tile([P, P], F32, name="ls_rows")
        ls_cols = keep.tile([P, BANKS], F32, name="ls_cols")
        ident = keep.tile([P, P], F32, name="ident")
        codes = keep.tile([P, T], U32, name="codes", align_bytes=64)
        gl_sc = keep.tile([P, T], U8, name="gl_sc", align_bytes=64)
        acc = [psum.tile([P, T], F32, name=f"acc{b}") for b in range(BANKS)]

        nc.gpsimd.memset(wb_sc[:].bitcast(I32), 0)
        nc.vector.memset(gb_sc[:].bitcast(I32), 0)
        nc.vector.memset(ls_rows[:], 0.0)
        nc.vector.memset(wo_sc[:].bitcast(I32), 0)
        make_identity(nc, ident[:])

        def load_rows(i):
            nc.sync.dma_start(rows[i][:], gt[P * i : P * (i + 1), :])

        def load_scales(queue, plane, src, r):
            queue.dma_start(plane[r:P:32].bitcast(I32), src[:, r:16:4, :].rearrange("z q c -> q z c").bitcast(I32))

        def load_wb(z):
            nc.sync.dma_start(wb_sb[z][:], wb_words[z].rearrange("p n t -> p (n t)").bitcast(I32))

        def load_gb(z):
            nc.sync.dma_start(gb_sb[z][:].bitcast(I32), gb_words[z].bitcast(I32))

        def load_base(z):
            load_wb(z)
            load_gb(z)

        load_wb(0)
        for r in range(2):
            load_scales(nc.sync, wb_sc, wb_scales, r)
        load_gb(0)
        load_rows(0)
        nc.sync.dma_start(offsets[:], offs)
        for r in range(2, 4):
            load_scales(nc.sync, wb_sc, wb_scales, r)
        for r in range(2):
            load_scales(nc.sync, gb_sc, gb_scales, r)
        load_rows(1)
        for r in range(2, 4):
            load_scales(nc.sync, gb_sc, gb_scales, r)
        load_rows(2)
        load_base(1)
        load_rows(3)
        load_base(2)
        load_base(3)
        nc.sync.dma_start(wo_sb[:].bitcast(I32), wo_words[0].bitcast(I32))
        for b in range(BANKS):
            nc.sync.dma_start(res_sb[b][:], res[P * b : P * (b + 1), :])
        nc.gpsimd.dma_start(ls_rows[8 : 8 + BANKS, :], ls.rearrange("(b c) o -> b (c o)", b=BANKS))
        for r in range(4):
            load_scales(nc.gpsimd, wo_sc, wo_scales, r)

        woven = [keep.tile([P, 2, 4 * P], BF16, name=f"woven{h}", align_bytes=64) for h in range(TILES // 2)]

        def listed(i):
            picked = keep.tile([P, J], BF16, name=f"picked{i}")
            nc.vector.tensor_copy(picked[:], rows[i][:].indirect(offsets[:]))
            pairs = picked[:].bitcast(F32)
            turned = psum.tile([P, 2, P], F32, name=f"turned{i % 2}")
            for u in range(2):
                nc.tensor.transpose(turned[:, u, :], pairs[:, u : J // 2 : 2], ident[:])
            half = woven[i // 2]
            nc.scalar.copy(half[:, i % 2, :].bitcast(F32).rearrange("p (r u) -> p r u", u=2), turned[:].rearrange("p u r -> p r u"))
            if i % 2 == 1:
                cols = slice(P * (i - 1), P * (i + 1))
                nc.vector.quantize_mx(out=codes[:, cols].bitcast(E5M2X4), scales=gl_sc[:, cols], in_=half[:].rearrange("p a c -> p (a c)"))

        def base_matmul(z, b):
            cols = slice(P * b, P * (b + 1))
            nc.tensor.matmul_mx(
                out=acc[b][:],
                lhsT=wb_sb[z][:, cols].bitcast(E4M3X4),
                lhsT_scale=wb_sc[:, z, cols],
                rhs=gb_sb[z][:].bitcast(E2M1X4),
                rhs_scale=gb_sc[:, z, :],
                start=(z == 0),
                stop=False,
            )

        for i in range(TILES):
            listed(i)
        ls_turned = psum.tile([P, P], F32, name="ls_turned")
        nc.tensor.transpose(ls_turned[:], ls_rows[:], ident[:])
        nc.scalar.copy(ls_cols[:], ls_turned[:, 8 : 8 + BANKS])
        for z in range(EARLY):
            for b in range(BANKS):
                base_matmul(z, b)

        for b in range(BANKS):
            cols = slice(P * b, P * (b + 1))
            for z in range(EARLY, PASSES):
                base_matmul(z, b)
            nc.tensor.matmul_mx(
                out=acc[b][:],
                lhsT=wo_sb[:, 2 * P * b : 2 * P * (b + 1)].bitcast(E2M1X4),
                lhsT_scale=wo_sc[:, 0, cols],
                rhs=codes[:].bitcast(E5M2X4),
                rhs_scale=gl_sc[:],
                start=False,
                stop=True,
            )
            pieces = 2 if b in (0, BANKS - 1) else 1
            width = T // pieces
            for h in range(pieces):
                tok = slice(width * h, width * (h + 1))
                result = keep.tile([P, width], F32, name=f"result{b}_{h}")
                nc.vector.scalar_tensor_tensor(result[:], acc[b][:, tok], ls_cols[:, b : b + 1], res_sb[b][:, tok], MULT, ADD)
                nc.sync.dma_start(out[cols, tok], result[:])
